import numpy as np, ml_dtypes
CORES = [0,4,8,12,16,20,24,28]
N = 8
def setup_inputs(rng):
    return {"x1": rng.standard_normal((N, 128, 8), dtype=np.float32), "x2": rng.standard_normal((N, 128, 2048), dtype=np.float32).astype(ml_dtypes.bfloat16)}
def reference(x1, x2):
    out = []
    b = 8 // N
    bl = x1.reshape(N, 128, N, b)
    out.append(np.ascontiguousarray(bl.transpose(2, 1, 0, 3)).reshape(N, 128, 8))
    s = x2.sum(axis=0, dtype=np.float64).astype(x2.dtype)
    out.append(np.broadcast_to(s, (N,) + s.shape))
    return {"y1": out[0], "y2": out[1]}

@@ -1,0 +1,115 @@
+from concourse.bass import RemoteDMATransfer, DstId
+
+NCH = 2
+W = 128 // NCH
+P = (2, 3, 6, 7)
+
+SCRATCH = {
+    "xs1": ("sbuf", [128, 8], "float32"),
+    "hx1": ("sbuf", [128, 8], "float32"),
+    "land1": ("sbuf", [128, 8], "float32"),
+    "xs": ("dram", [16 * NCH, 128, W], "bfloat16"),
+    "la": ("dram", [4 * NCH, 128, W], "bfloat16"),
+    "lb": ("dram", [4 * NCH, 128, W], "bfloat16"),
+    "part": ("dram", [4 * NCH, 128, W], "bfloat16"),
+    "fin": ("dram", [16 * NCH, 128, W], "bfloat16"),
+}
+SEMAPHORES = ["l1", "g1", "a1", "st", "sent",
+              "ld0", "ld1", "ld2", "ld3", "ha0", "ha1", "ha2", "ha3",
+              "hb0", "hb1", "hb2", "hb3", "hc0", "hc1", "hc2", "hc3"]
+
+
+def rank_program(g, core, T, topo):
+    chip, k = divmod(core, 8)
+    S = T.sem
+    ld = [S.ld0, S.ld1, S.ld2, S.ld3]
+    h1 = [S.ha0, S.ha1, S.ha2, S.ha3]
+    h2 = [S.hb0, S.hb1, S.hb2, S.hb3]
+    h3 = [S.hc0, S.hc1, S.hc2, S.hc3]
+    sent = 0
+
+    def did(c):
+        rid, pid, se = topo.addr(c)
+        return DstId(rid=rid, pnc=pid)
+
+    if k in (0, 4):
+        rows = 128 // NCH
+        g.dma_start(T.xs1[:], T.x1[:]).then_inc(S.l1, 16)
+        for c in range(NCH):
+            g.dma_start(T.xs[16 * c:16 * c + 16], T.x2[rows * c:rows * (c + 1), :]).then_inc(ld[c], 16)
+        g.wait_ge(S.l1, 16)
+        g.remote_dma_fused([RemoteDMATransfer(
+            dst_ids=[did(core + 1), did(core + 2), did(core + 3)], dma_engine_mask=0xFFFF, remote_sem=S.g1,
+            srcs=[T.xs1[:]], dsts=[T.hx1[:], T.hx1[:], T.hx1[:]], alu_op=0)], local_sem=S.sent)
+        sent += 16
+        land = T.la if k == 0 else T.lb
+        for c in range(NCH):
+            g.wait_ge(ld[c], 16)
+            trs = []
+            for d in range(4):
+                for i in range(4):
+                    if d == chip ^ 2:
+                        helper, slot = 8 * chip + (1 if i < 2 else 5), i % 2
+                    else:
+                        helper, slot = 8 * chip + P[i], d
+                    trs.append(RemoteDMATransfer(
+                        dst_ids=[did(helper)], dma_engine_mask=1 << (4 * d + i), remote_sem=h1[c],
+                        src=T.xs[16 * c + 4 * d + i], dst=land[4 * c + slot]))
+            g.remote_dma_fused(trs, local_sem=S.sent)
+            sent += 16
+        g.wait_ge(S.a1, 32)
+        g.dma_start(T.y1[:], T.land1[:]).then_inc(S.st, 16)
+        for c in range(NCH):
+            g.wait_ge(h3[c], 128)
+            g.dma_start(T.y2[rows * c:rows * (c + 1), :], T.fin[16 * c:16 * c + 16]).then_inc(S.st, 16)
+        g.wait_ge(S.st, 16 * (NCH + 1))
+        g.wait_ge(S.sent, sent)
+        return
+
+    base = core - k % 4
+    r = T.rank_of(base)
+    if k % 4 == 1:
+        dests = [(base, 0x0F00), (base ^ 4, 0xF000), (8 * (chip ^ 2), 0x000F), (8 * (chip ^ 2) + 4, 0x00F0)]
+    else:
+        d = chip ^ 1 if k % 4 == 2 else chip ^ 3
+        dests = [(8 * d, 0x000F), (8 * d + 4, 0x00F0)]
+    g.wait_ge(S.g1, 16)
+    g.remote_dma_fused([RemoteDMATransfer(
+        dst_ids=[did(dc)], dma_engine_mask=m, remote_sem=S.a1,
+        src=T.hx1[:, T.rank_of(dc):T.rank_of(dc) + 1], dst=T.land1[:, r:r + 1]) for dc, m in dests],
+        local_sem=S.sent)
+    sent += 4 * len(dests)
+
+    if k % 4 == 1:
+        d = chip ^ 2
+        for c in range(NCH):
+            g.wait_ge(h1[c], 4)
+            g.remote_dma_fused([RemoteDMATransfer(
+                dst_ids=[did(8 * d + P[i])], dma_engine_mask=0xF << (4 * (i % 2)), remote_sem=h2[c],
+                srcs=[T.la[4 * c + i % 2], T.lb[4 * c + i % 2]], dsts=[T.part[4 * c + chip]], alu_op=1)
+                for i in ((0, 1) if k == 1 else (2, 3))], local_sem=S.sent)
+            sent += 8
+        g.wait_ge(S.sent, sent)
+        return
+
+    i = P.index(k)
+    for c in range(NCH):
+        g.wait_ge(h1[c], 6)
+        g.remote_dma_fused([RemoteDMATransfer(
+            dst_ids=[did(8 * d + k)], dma_engine_mask=0xF << (4 * n), remote_sem=h2[c],
+            srcs=[T.la[4 * c + d], T.lb[4 * c + d]], dsts=[T.part[4 * c + chip]], alu_op=1)
+            for n, d in enumerate((chip ^ 1, chip ^ 3))], local_sem=S.sent)
+        sent += 8
+    for c in range(NCH):
+        g.wait_ge(h2[c], 12)
+        srcs = [T.la[4 * c + chip], T.lb[4 * c + chip]] + [T.part[4 * c + d] for d in range(4) if d != chip]
+        out = T.fin[16 * c + 4 * chip + i]
+        near = [8 * chip, 8 * chip + 4]
+        far = [8 * d + q for d in range(4) if d != chip for q in (0, 4)]
+        g.remote_dma_fused([
+            RemoteDMATransfer(dst_ids=[did(x) for x in far], dma_engine_mask=0x00FF, remote_sem=h3[c],
+                              srcs=srcs, dsts=[out for x in far], alu_op=1),
+            RemoteDMATransfer(dst_ids=[did(x) for x in near], dma_engine_mask=0xFF00, remote_sem=h3[c],
+                              srcs=srcs, dsts=[out for x in near], alu_op=1)], local_sem=S.sent)
+        sent += 16
+    g.wait_ge(S.sent, sent)

@@ -1,6 +1,7 @@
 from concourse.bass import RemoteDMATransfer, DstId
 
 NCH = 2
+RELAY = True
 W = 128 // NCH
 P = (2, 3, 6, 7)
 
@@ -12,11 +13,12 @@ SCRATCH = {
     "la": ("dram", [4 * NCH, 128, W], "bfloat16"),
     "lb": ("dram", [4 * NCH, 128, W], "bfloat16"),
     "part": ("dram", [4 * NCH, 128, W], "bfloat16"),
+    "rl": ("dram", [4 * NCH, 128, W], "bfloat16"),
     "fin": ("dram", [16 * NCH, 128, W], "bfloat16"),
 }
 SEMAPHORES = ["l1", "g1", "a1", "st", "sent",
               "ld0", "ld1", "ld2", "ld3", "ha0", "ha1", "ha2", "ha3",
-              "hb0", "hb1", "hb2", "hb3", "hc0", "hc1", "hc2", "hc3"]
+              "hb0", "hb1", "hb2", "hb3", "hc0", "hc1", "hc2", "hc3", "hd0", "hd1", "hd2", "hd3"]
 
 
 def rank_program(g, core, T, topo):
@@ -26,6 +28,7 @@ def rank_program(g, core, T, topo):
     h1 = [S.ha0, S.ha1, S.ha2, S.ha3]
     h2 = [S.hb0, S.hb1, S.hb2, S.hb3]
     h3 = [S.hc0, S.hc1, S.hc2, S.hc3]
+    h4 = [S.hd0, S.hd1, S.hd2, S.hd3]
     sent = 0
 
     def did(c):
@@ -60,7 +63,7 @@ def rank_program(g, core, T, topo):
         g.wait_ge(S.a1, 32)
         g.dma_start(T.y1[:], T.land1[:]).then_inc(S.st, 16)
         for c in range(NCH):
-            g.wait_ge(h3[c], 128)
+            g.wait_ge(h3[c], 4 * 8 + 12 * 4 if RELAY else 128)
             g.dma_start(T.y2[rows * c:rows * (c + 1), :], T.fin[16 * c:16 * c + 16]).then_inc(S.st, 16)
         g.wait_ge(S.st, 16 * (NCH + 1))
         g.wait_ge(S.sent, sent)
@@ -93,6 +96,8 @@ def rank_program(g, core, T, topo):
         return
 
     i = P.index(k)
+    others = [d for d in range(4) if d != chip]
+    near = [8 * chip, 8 * chip + 4]
     for c in range(NCH):
         g.wait_ge(h1[c], 6)
         g.remote_dma_fused([RemoteDMATransfer(
@@ -102,14 +107,25 @@ def rank_program(g, core, T, topo):
         sent += 8
     for c in range(NCH):
         g.wait_ge(h2[c], 12)
-        srcs = [T.la[4 * c + chip], T.lb[4 * c + chip]] + [T.part[4 * c + d] for d in range(4) if d != chip]
+        srcs = [T.la[4 * c + chip], T.lb[4 * c + chip]] + [T.part[4 * c + d] for d in others]
         out = T.fin[16 * c + 4 * chip + i]
-        near = [8 * chip, 8 * chip + 4]
-        far = [8 * d + q for d in range(4) if d != chip for q in (0, 4)]
-        g.remote_dma_fused([
-            RemoteDMATransfer(dst_ids=[did(x) for x in far], dma_engine_mask=0x00FF, remote_sem=h3[c],
-                              srcs=srcs, dsts=[out for x in far], alu_op=1),
-            RemoteDMATransfer(dst_ids=[did(x) for x in near], dma_engine_mask=0xFF00, remote_sem=h3[c],
-                              srcs=srcs, dsts=[out for x in near], alu_op=1)], local_sem=S.sent)
+        if RELAY:
+            far = RemoteDMATransfer(dst_ids=[did(8 * d + k) for d in others], dma_engine_mask=0x00FF,
+                                    remote_sem=h4[c], srcs=srcs, dsts=[T.rl[4 * c + chip] for d in others], alu_op=1)
+        else:
+            fc = [8 * d + q for d in others for q in (0, 4)]
+            far = RemoteDMATransfer(dst_ids=[did(x) for x in fc], dma_engine_mask=0x00FF, remote_sem=h3[c],
+                                    srcs=srcs, dsts=[out for x in fc], alu_op=1)
+        g.remote_dma_fused([far, RemoteDMATransfer(
+            dst_ids=[did(x) for x in near], dma_engine_mask=0xFF00, remote_sem=h3[c],
+            srcs=srcs, dsts=[out for x in near], alu_op=1)], local_sem=S.sent)
         sent += 16
+    if RELAY:
+        for c in range(NCH):
+            g.wait_ge(h4[c], 24)
+            g.remote_dma_fused([RemoteDMATransfer(
+                dst_ids=[did(x) for x in near], dma_engine_mask=0xF << (4 * n), remote_sem=h3[c],
+                srcs=[T.rl[4 * c + d]], dsts=[T.fin[16 * c + 4 * d + i] for x in near], alu_op=0)
+                for n, d in enumerate(others)], local_sem=S.sent)
+            sent += 12
     g.wait_ge(S.sent, sent)

@@ -1,7 +1,6 @@
 from concourse.bass import RemoteDMATransfer, DstId
 
 NCH = 2
-RELAY = True
 W = 128 // NCH
 P = (2, 3, 6, 7)
 
@@ -16,19 +15,13 @@ SCRATCH = {
     "rl": ("dram", [4 * NCH, 128, W], "bfloat16"),
     "fin": ("dram", [16 * NCH, 128, W], "bfloat16"),
 }
-SEMAPHORES = ["l1", "g1", "a1", "st", "sent",
-              "ld0", "ld1", "ld2", "ld3", "ha0", "ha1", "ha2", "ha3",
-              "hb0", "hb1", "hb2", "hb3", "hc0", "hc1", "hc2", "hc3", "hd0", "hd1", "hd2", "hd3"]
+SEMAPHORES = ["l1", "g1", "a1", "st", "sent", "ld0", "ld1", "ha0", "ha1", "hb0", "hb1", "hc0", "hc1", "hd0", "hd1"]
 
 
 def rank_program(g, core, T, topo):
     chip, k = divmod(core, 8)
     S = T.sem
-    ld = [S.ld0, S.ld1, S.ld2, S.ld3]
-    h1 = [S.ha0, S.ha1, S.ha2, S.ha3]
-    h2 = [S.hb0, S.hb1, S.hb2, S.hb3]
-    h3 = [S.hc0, S.hc1, S.hc2, S.hc3]
-    h4 = [S.hd0, S.hd1, S.hd2, S.hd3]
+    ld, h1, h2, h3, h4 = [S.ld0, S.ld1], [S.ha0, S.ha1], [S.hb0, S.hb1], [S.hc0, S.hc1], [S.hd0, S.hd1]
     sent = 0
 
     def did(c):
@@ -63,7 +56,7 @@ def rank_program(g, core, T, topo):
         g.wait_ge(S.a1, 32)
         g.dma_start(T.y1[:], T.land1[:]).then_inc(S.st, 16)
         for c in range(NCH):
-            g.wait_ge(h3[c], 4 * 8 + 12 * 4 if RELAY else 128)
+            g.wait_ge(h3[c], 4 * 8 + 12 * 4)
             g.dma_start(T.y2[rows * c:rows * (c + 1), :], T.fin[16 * c:16 * c + 16]).then_inc(S.st, 16)
         g.wait_ge(S.st, 16 * (NCH + 1))
         g.wait_ge(S.sent, sent)
@@ -108,24 +101,18 @@ def rank_program(g, core, T, topo):
     for c in range(NCH):
         g.wait_ge(h2[c], 12)
         srcs = [T.la[4 * c + chip], T.lb[4 * c + chip]] + [T.part[4 * c + d] for d in others]
-        out = T.fin[16 * c + 4 * chip + i]
-        if RELAY:
-            far = RemoteDMATransfer(dst_ids=[did(8 * d + k) for d in others], dma_engine_mask=0x00FF,
-                                    remote_sem=h4[c], srcs=srcs, dsts=[T.rl[4 * c + chip] for d in others], alu_op=1)
-        else:
-            fc = [8 * d + q for d in others for q in (0, 4)]
-            far = RemoteDMATransfer(dst_ids=[did(x) for x in fc], dma_engine_mask=0x00FF, remote_sem=h3[c],
-                                    srcs=srcs, dsts=[out for x in fc], alu_op=1)
-        g.remote_dma_fused([far, RemoteDMATransfer(
-            dst_ids=[did(x) for x in near], dma_engine_mask=0xFF00, remote_sem=h3[c],
-            srcs=srcs, dsts=[out for x in near], alu_op=1)], local_sem=S.sent)
+        g.remote_dma_fused([
+            RemoteDMATransfer(dst_ids=[did(8 * d + k) for d in others], dma_engine_mask=0x00FF, remote_sem=h4[c],
+                              srcs=srcs, dsts=[T.rl[4 * c + chip] for d in others], alu_op=1),
+            RemoteDMATransfer(dst_ids=[did(x) for x in near], dma_engine_mask=0xFF00, remote_sem=h3[c],
+                              srcs=srcs, dsts=[T.fin[16 * c + 4 * chip + i] for x in near], alu_op=1)],
+            local_sem=S.sent)
         sent += 16
-    if RELAY:
-        for c in range(NCH):
-            g.wait_ge(h4[c], 24)
-            g.remote_dma_fused([RemoteDMATransfer(
-                dst_ids=[did(x) for x in near], dma_engine_mask=0xF << (4 * n), remote_sem=h3[c],
-                srcs=[T.rl[4 * c + d]], dsts=[T.fin[16 * c + 4 * d + i] for x in near], alu_op=0)
-                for n, d in enumerate(others)], local_sem=S.sent)
-            sent += 12
+    for c in range(NCH):
+        g.wait_ge(h4[c], 24)
+        g.remote_dma_fused([RemoteDMATransfer(
+            dst_ids=[did(x) for x in near], dma_engine_mask=0xF << (4 * n), remote_sem=h3[c],
+            srcs=[T.rl[4 * c + d]], dsts=[T.fin[16 * c + 4 * d + i] for x in near], alu_op=0)
+            for n, d in enumerate(others)], local_sem=S.sent)
+        sent += 12
     g.wait_ge(S.sent, sent)

from concourse.bass import RemoteDMATransfer, DstId

NCH = 2
W = 128 // NCH
P = (2, 3, 6, 7)

SCRATCH = {
    "xs1": ("sbuf", [128, 8], "float32"),
    "hx1": ("sbuf", [128, 8], "float32"),
    "land1": ("sbuf", [128, 8], "float32"),
    "xs": ("dram", [16 * NCH, 128, W], "bfloat16"),
    "la": ("dram", [4 * NCH, 128, W], "bfloat16"),
    "lb": ("dram", [4 * NCH, 128, W], "bfloat16"),
    "part": ("dram", [4 * NCH, 128, W], "bfloat16"),
    "rl": ("dram", [4 * NCH, 128, W], "bfloat16"),
    "fin": ("dram", [16 * NCH, 128, W], "bfloat16"),
}
SEMAPHORES = ["l1", "g1", "a1", "st", "sent", "ld0", "ld1", "ha0", "ha1", "hb0", "hb1", "hc0", "hc1", "hd0", "hd1"]


def rank_program(g, core, T, topo):
    chip, k = divmod(core, 8)
    S = T.sem
    ld, h1, h2, h3, h4 = [S.ld0, S.ld1], [S.ha0, S.ha1], [S.hb0, S.hb1], [S.hc0, S.hc1], [S.hd0, S.hd1]
    sent = 0

    def did(c):
        rid, pid, se = topo.addr(c)
        return DstId(rid=rid, pnc=pid)

    if k in (0, 4):
        rows = 128 // NCH
        g.dma_start(T.xs1[:], T.x1[:]).then_inc(S.l1, 16)
        for c in range(NCH):
            g.dma_start(T.xs[16 * c:16 * c + 16], T.x2[rows * c:rows * (c + 1), :]).then_inc(ld[c], 16)
        g.wait_ge(S.l1, 16)
        g.remote_dma_fused([RemoteDMATransfer(
            dst_ids=[did(core + 1), did(core + 2), did(core + 3)], dma_engine_mask=0xFFFF, remote_sem=S.g1,
            srcs=[T.xs1[:]], dsts=[T.hx1[:], T.hx1[:], T.hx1[:]], alu_op=0)], local_sem=S.sent)
        sent += 16
        land = T.la if k == 0 else T.lb
        for c in range(NCH):
            g.wait_ge(ld[c], 16)
            trs = []
            for d in range(4):
                for i in range(4):
                    if d == chip ^ 2:
                        helper, slot = 8 * chip + (1 if i < 2 else 5), i % 2
                    else:
                        helper, slot = 8 * chip + P[i], d
                    trs.append(RemoteDMATransfer(
                        dst_ids=[did(helper)], dma_engine_mask=1 << (4 * d + i), remote_sem=h1[c],
                        src=T.xs[16 * c + 4 * d + i], dst=land[4 * c + slot]))
            g.remote_dma_fused(trs, local_sem=S.sent)
            sent += 16
        g.wait_ge(S.a1, 32)
        g.dma_start(T.y1[:], T.land1[:]).then_inc(S.st, 16)
        for c in range(NCH):
            g.wait_ge(h3[c], 4 * 8 + 12 * 4)
            g.dma_start(T.y2[rows * c:rows * (c + 1), :], T.fin[16 * c:16 * c + 16]).then_inc(S.st, 16)
        g.wait_ge(S.st, 16 * (NCH + 1))
        g.wait_ge(S.sent, sent)
        return

    base = core - k % 4
    r = T.rank_of(base)
    if k % 4 == 1:
        dests = [(base, 0x0F00), (base ^ 4, 0xF000), (8 * (chip ^ 2), 0x000F), (8 * (chip ^ 2) + 4, 0x00F0)]
    else:
        d = chip ^ 1 if k % 4 == 2 else chip ^ 3
        dests = [(8 * d, 0x000F), (8 * d + 4, 0x00F0)]
    g.wait_ge(S.g1, 16)
    g.remote_dma_fused([RemoteDMATransfer(
        dst_ids=[did(dc)], dma_engine_mask=m, remote_sem=S.a1,
        src=T.hx1[:, T.rank_of(dc):T.rank_of(dc) + 1], dst=T.land1[:, r:r + 1]) for dc, m in dests],
        local_sem=S.sent)
    sent += 4 * len(dests)

    if k % 4 == 1:
        d = chip ^ 2
        for c in range(NCH):
            g.wait_ge(h1[c], 4)
            g.remote_dma_fused([RemoteDMATransfer(
                dst_ids=[did(8 * d + P[i])], dma_engine_mask=0xF << (4 * (i % 2)), remote_sem=h2[c],
                srcs=[T.la[4 * c + i % 2], T.lb[4 * c + i % 2]], dsts=[T.part[4 * c + chip]], alu_op=1)
                for i in ((0, 1) if k == 1 else (2, 3))], local_sem=S.sent)
            sent += 8
        g.wait_ge(S.sent, sent)
        return

    i = P.index(k)
    others = [d for d in range(4) if d != chip]
    near = [8 * chip, 8 * chip + 4]
    for c in range(NCH):
        g.wait_ge(h1[c], 6)
        g.remote_dma_fused([RemoteDMATransfer(
            dst_ids=[did(8 * d + k)], dma_engine_mask=0xF << (4 * n), remote_sem=h2[c],
            srcs=[T.la[4 * c + d], T.lb[4 * c + d]], dsts=[T.part[4 * c + chip]], alu_op=1)
            for n, d in enumerate((chip ^ 1, chip ^ 3))], local_sem=S.sent)
        sent += 8
    for c in range(NCH):
        g.wait_ge(h2[c], 12)
        srcs = [T.la[4 * c + chip], T.lb[4 * c + chip]] + [T.part[4 * c + d] for d in others]
        g.remote_dma_fused([
            RemoteDMATransfer(dst_ids=[did(8 * d + k) for d in others], dma_engine_mask=0x00FF, remote_sem=h4[c],
                              srcs=srcs, dsts=[T.rl[4 * c + chip] for d in others], alu_op=1),
            RemoteDMATransfer(dst_ids=[did(x) for x in near], dma_engine_mask=0xFF00, remote_sem=h3[c],
                              srcs=srcs, dsts=[T.fin[16 * c + 4 * chip + i] for x in near], alu_op=1)],
            local_sem=S.sent)
        sent += 16
    for c in range(NCH):
        g.wait_ge(h4[c], 24)
        g.remote_dma_fused([RemoteDMATransfer(
            dst_ids=[did(x) for x in near], dma_engine_mask=0xF << (4 * n), remote_sem=h3[c],
            srcs=[T.rl[4 * c + d]], dsts=[T.fin[16 * c + 4 * d + i] for x in near], alu_op=0)
            for n, d in enumerate(others)], local_sem=S.sent)
        sent += 12
    g.wait_ge(S.sent, sent)
